import numpy as np
import ml_dtypes


def mxq(x, axis, fmt="e4m3"):
    dtype, down = {"e4m3": (ml_dtypes.float8_e4m3fn, 7), "e5m2": (ml_dtypes.float8_e5m2, 14)}[fmt]
    v = np.moveaxis(np.asarray(x, np.float32).astype(ml_dtypes.bfloat16).astype(np.float64), axis, -1)
    blocks = v.reshape(v.shape[:-1] + (-1, 32))
    amax = np.abs(blocks).max(-1, keepdims=True)
    byte = np.maximum(np.where(amax > 0, np.frexp(amax)[1] - 1 + 127, 0) - down, 1)
    scale = np.exp2(byte - 127.0)
    codes = (blocks / scale).astype(np.float32).astype(dtype).astype(np.float64)
    return np.moveaxis((codes * scale).reshape(v.shape), -1, axis)


WIDE = False


def mx_kscale(k, group=512):
    if not WIDE:
        return np.ones(k)
    levels = np.array([18, -18])
    if group != 512:
        return np.exp2(np.random.permutation(np.resize(levels, k // group))).repeat(group)
    if k % 512:
        return np.exp2(np.random.permutation(np.resize(levels, k // 32))).repeat(32)
    a = np.empty((k // 512, 16))
    for p in range(k // 512):
        a[p, :8] = np.random.permutation(np.resize(levels, 8))
        for g in range(8):
            far = levels[np.abs(levels - a[p, g]) >= 10]
            a[p, g + 8] = far[np.random.randint(len(far))]
    return np.exp2(a.ravel()).repeat(32)


def f64(x):
    return np.asarray(x).astype(np.float64)


def sigmoid(v):
    return 1.0 / (1.0 + np.exp(-v))


def bf(x):
    return np.asarray(x, np.float32).astype(ml_dtypes.bfloat16)


def planes(Y):
    r, m = Y.shape
    b = f64(bf(Y)).reshape(r // 32, 32, m)
    amax = np.abs(b).max(1)
    byte = np.clip(np.where(amax > 0, np.frexp(amax)[1] - 1 + 127 - 7, 1), 1, 254)
    codes = (b * np.exp2(127.0 - byte)[:, None, :]).reshape(r, m).astype(np.float32).astype(ml_dtypes.float8_e4m3fn).view(np.uint8)
    words = codes.reshape(r // 512, 128, 4, m).transpose(0, 1, 3, 2)
    return np.ascontiguousarray(words), np.ascontiguousarray(byte.astype(np.uint8).reshape(r // 512, 16, m))


G, D, M, N = 4, 128, 128, 512


def setup_inputs():
    n = np.random.standard_normal
    s_d = mx_kscale(D, 0)
    return {
        "h": (n((G, D, N)) * s_d[:, None]).astype(np.float32),
        "wi": (n((G, D, M)) / np.sqrt(D) / s_d[:, None]).astype(np.float32),
        "wf": (n((G, D, M)) / np.sqrt(D) / s_d[:, None]).astype(np.float32),
        "wo": (n((G, D, M)) / np.sqrt(D) / s_d[:, None]).astype(np.float32),
        "wc": (n((G, D, M)) / np.sqrt(D) / s_d[:, None]).astype(np.float32),
        "xi": (n((G, M, N))).astype(np.float32),
        "xf": (n((G, M, N))).astype(np.float32),
        "xo": (n((G, M, N))).astype(np.float32),
        "xc": (n((G, M, N))).astype(np.float32),
        "c": (n((G, M, N))).astype(np.float32),
    }


def reference(h, wi, wf, wo, wc, xi, xf, xo, xc, c):
    wiq = mxq(f64(wi), 1, "e4m3")
    hq = mxq(f64(h), 1, "e4m3")
    zi = wiq.transpose(0, 2, 1) @ hq
    wfq = mxq(f64(wf), 1, "e4m3")
    zf = wfq.transpose(0, 2, 1) @ hq
    woq = mxq(f64(wo), 1, "e4m3")
    zo = woq.transpose(0, 2, 1) @ hq
    wcq = mxq(f64(wc), 1, "e4m3")
    zc = wcq.transpose(0, 2, 1) @ hq
    cn = sigmoid(zf + f64(xf)) * f64(c) + sigmoid(zi + f64(xi)) * np.tanh(zc + f64(xc))
    y = sigmoid(zo + f64(xo)) * np.tanh(cn)
    Y = y.reshape(G * M, N)
    words, scales = planes(Y)
    return Y, words, scales

@@ -1,0 +1,257 @@
+from contextlib import ExitStack
+
+import concourse.mybir as mybir
+
+G, D, M, N = 4, 128, 128, 512
+FLOPS = 2 * 4 * G * D * M * N
+
+F32 = mybir.dt.float32
+BF16 = mybir.dt.bfloat16
+U32 = mybir.dt.uint32
+I32 = mybir.dt.int32
+U8 = mybir.dt.uint8
+FP8X4 = mybir.dt.float8_e4m3fn_x4
+ACT = mybir.ActivationFunctionType
+ALU = mybir.AluOpType
+
+P = 128
+PACK = 4
+ROWS = D // PACK
+QUARTER = N // 4
+HALF = N // 2
+
+
+def tile_rows_pl_cell_lstm_kernel(tc, h, wi, wf, wo, wc, xi, xf, xo, xc, c, out_0, out_1, out_2):
+    nc = tc.nc
+    weights = {"f": wf, "i": wi, "c": wc, "o": wo}
+    addends = {"f": xf, "i": xi, "c": xc, "o": xo, "cell": c}
+    bank_of = {"f": 0, "i": 1, "c": 0, "o": 1}
+    func_of = {"f": ACT.Sigmoid, "i": ACT.Sigmoid, "c": ACT.Tanh, "o": ACT.Sigmoid}
+    words_hbm = out_1.rearrange("s p n t -> (s p) (n t)").bitcast(I32)
+    scales_hbm = out_2.rearrange("s (g b) n -> (s b) g n", b=4).bitcast(I32)
+
+    with ExitStack() as ctx:
+        keep = ctx.enter_context(tc.tile_pool(name="keep", bufs=1))
+        psum = ctx.enter_context(tc.psum_pool(name="psum", bufs=1))
+        ctx.enter_context(tc.manual_schedule())
+
+        def sbuf(name, shape, dtype, tag=""):
+            return keep.tile(shape, dtype, name=name, tag=tag or name, align_bytes=64)
+
+        banks = [[psum.tile([P, N], F32, name="bank%d%d" % (g, b)) for b in range(2)] for g in range(G)]
+        w_raw = {k: sbuf("w_raw_" + k, [P, PACK, M], F32) for k in weights}
+        w_bf = {k: sbuf("w_bf_" + k, [P, M, PACK], BF16) for k in weights}
+        w_codes = {k: sbuf("w_codes_" + k, [P, M], U32) for k in weights}
+        w_scales = {k: sbuf("w_scales_" + k, [P, M], U8) for k in weights}
+        h_raw = [sbuf("h_raw%d" % u, [P, PACK, HALF], F32) for u in range(2)]
+        h_bf = [sbuf("h_bf%d" % u, [P, HALF, PACK], BF16) for u in range(2)]
+        h_codes = sbuf("h_codes", [P, N], U32)
+        h_scales = sbuf("h_scales", [P, N], U8)
+        x_sb = {(k, g): sbuf("x_%s%d" % (k, g), [P, N], F32) for k in addends for g in range(G)}
+        pre = {(k, g): sbuf("pre_%s%d" % (k, g), [P, N], F32) for k in weights for g in range(G)}
+        gate = {(k, g): sbuf("gate_%s%d" % (k, g), [P, N], F32) for k in weights for g in range(G)}
+        cell_new = [sbuf("cell_new%d" % g, [P, N], F32) for g in range(G)]
+        y = [sbuf("y%d" % g, [P, N], F32) for g in range(G)]
+        y_rows = [sbuf("y_rows%d" % g, [P, PACK, QUARTER], F32) for g in range(G)]
+        y_bf = [sbuf("y_bf%d" % g, [P, QUARTER, PACK], BF16) for g in range(G)]
+        y_codes = [sbuf("y_codes%d" % g, [P, QUARTER], U32) for g in range(G)]
+        y_scales = sbuf("y_scales", [P, G, QUARTER], U8)
+        kept = sbuf("kept", [P, N], F32)
+        scratch = sbuf("scratch", [P, N], F32)
+        warm_in = sbuf("warm_in", [P, 8], F32)
+        warm_out = sbuf("warm_out", [P, 8], F32)
+
+        def load_w(k):
+            nc.sync.dma_start(out=w_raw[k][:], in_=weights[k].rearrange("g (p j) m -> (g p) j m", j=PACK))
+
+        def load_h(u):
+            rows = h.rearrange("g (p j) n -> (g p) j n", j=PACK)
+            nc.sync.dma_start(out=h_raw[u][:], in_=rows[:, :, u * HALF : (u + 1) * HALF])
+
+        def load_x(k, g):
+            nc.sync.dma_start(out=x_sb[k, g][:], in_=addends[k][g])
+
+        def interleave(copy, dst, src):
+            copy(
+                out=dst[:].rearrange("p (c i) t -> p c t i", i=4),
+                in_=src[:].rearrange("p t (c i) -> p c t i", i=4),
+            )
+
+        def quantize(codes, scales, src):
+            nc.vector.quantize_mx(
+                out=codes.bitcast(FP8X4), scales=scales, in_=src[:].rearrange("p n t -> p (n t)")
+            )
+
+        def quantize_w(k):
+            quantize(w_codes[k][:], w_scales[k][:], w_bf[k])
+
+        def quantize_h(u):
+            cols = slice(u * HALF, (u + 1) * HALF)
+            quantize(h_codes[:, cols], h_scales[:, cols], h_bf[u])
+
+        def product(k, g):
+            rows = slice(ROWS * g, ROWS * (g + 1))
+            nc.tensor.matmul_mx(
+                out=banks[g][bank_of[k]][:],
+                lhsT=w_codes[k][rows, :].bitcast(FP8X4),
+                lhsT_scale=w_scales[k][rows, :],
+                rhs=h_codes[rows, :].bitcast(FP8X4),
+                rhs_scale=h_scales[rows, :],
+                start=True,
+                stop=True,
+            )
+
+        def add_input(k, g):
+            nc.vector.tensor_tensor(out=pre[k, g][:], in0=banks[g][bank_of[k]][:], in1=x_sb[k, g][:], op=ALU.add)
+
+        def activate(k, g):
+            nc.scalar.activation(out=gate[k, g][:], in_=pre[k, g][:], func=func_of[k])
+
+        def keep_cell(g):
+            nc.gpsimd.tensor_tensor(out=kept[:], in0=gate["f", g][:], in1=x_sb["cell", g][:], op=ALU.mult)
+
+        def admit(engine, g, cols):
+            engine.tensor_tensor(out=scratch[:, cols], in0=gate["i", g][:, cols], in1=gate["c", g][:, cols], op=ALU.mult)
+
+        def new_cell(g, cols):
+            nc.vector.tensor_tensor(out=cell_new[g][:, cols], in0=kept[:, cols], in1=scratch[:, cols], op=ALU.add)
+
+        def squash(g, cols):
+            nc.scalar.activation(out=scratch[:, cols], in_=cell_new[g][:, cols], func=ACT.Tanh)
+
+        def emit(g, cols):
+            nc.vector.tensor_tensor(out=y[g][:, cols], in0=gate["o", g][:, cols], in1=scratch[:, cols], op=ALU.mult)
+
+        def regroup(g, a):
+            nc.sync.dma_start(
+                out=y_rows[g][ROWS * a : ROWS * (a + 1), :, :], in_=y[g][:, QUARTER * a : QUARTER * (a + 1)]
+            )
+
+        def store_y(g):
+            nc.sync.dma_start(out=out_0[M * g : M * (g + 1), :], in_=y[g][:])
+
+        def quantize_y(g):
+            quantize(y_codes[g][:], y_scales[:, g, :], y_bf[g])
+
+        def store_words(g):
+            dst = words_hbm[ROWS * g : ROWS * (g + 1), :].rearrange("p (a n) -> a p n", a=4)
+            nc.sync.dma_start(out=dst, in_=y_codes[g][:].bitcast(I32))
+
+        def store_words_quarter(g, a):
+            nc.sync.dma_start(
+                out=words_hbm[ROWS * g : ROWS * (g + 1), QUARTER * a : QUARTER * (a + 1)],
+                in_=y_codes[g][:].bitcast(I32)[ROWS * a : ROWS * (a + 1), :],
+            )
+
+        def store_scales(a):
+            width = QUARTER // 4
+            nc.scalar.dma_start(
+                out=scales_hbm[:, :, width * a : width * (a + 1)],
+                in_=y_scales[:].bitcast(I32)[ROWS * a : ROWS * a + 4, :, :],
+            )
+
+        whole = slice(0, N)
+        halves = [slice(0, HALF), slice(HALF, N)]
+        order = ["f", "i", "c", "cell", "o"]
+
+        nc.gpsimd.memset(warm_in[:], 0.0)
+        nc.scalar.activation(out=warm_out[:], in_=warm_in[:], func=ACT.Sigmoid)
+
+        load_w("f")
+        load_h(0)
+        load_h(1)
+        load_w("i")
+        load_x("f", 0)
+        load_w("c")
+        load_x("i", 0)
+        load_w("o")
+        for k in order[2:]:
+            load_x(k, 0)
+        for g in (1, 2):
+            for k in order:
+                load_x(k, g)
+        load_x("f", 3)
+
+        interleave(nc.vector.tensor_copy, w_bf["f"], w_raw["f"])
+        quantize_w("f")
+        interleave(nc.vector.tensor_copy, h_bf[0], h_raw[0])
+        quantize_h(0)
+        interleave(nc.vector.tensor_copy, h_bf[1], h_raw[1])
+        interleave(nc.scalar.copy, w_bf["i"], w_raw["i"])
+        quantize_h(1)
+        quantize_w("i")
+        for g in (0, 1):
+            product("f", g)
+            product("i", g)
+
+        interleave(nc.scalar.copy, w_bf["c"], w_raw["c"])
+        add_input("f", 0)
+        activate("f", 0)
+        quantize_w("c")
+        product("c", 0)
+        interleave(nc.scalar.copy, w_bf["o"], w_raw["o"])
+        add_input("i", 0)
+        activate("i", 0)
+        quantize_w("o")
+        product("o", 0)
+        keep_cell(0)
+        for k in ("c", "o"):
+            add_input(k, 0)
+            activate(k, 0)
+        admit(nc.gpsimd, 0, whole)
+
+        for g in range(1, G):
+            if g + 1 < G:
+                product("f", g + 1)
+                product("i", g + 1)
+            add_input("f", g)
+            activate("f", g)
+            product("c", g)
+            add_input("i", g)
+            activate("i", g)
+            product("o", g)
+            if g == 3:
+                quantize_y(0)
+            new_cell(g - 1, whole)
+            squash(g - 1, whole)
+            keep_cell(g)
+            for k in ("c", "o"):
+                add_input(k, g)
+                activate(k, g)
+            emit(g - 1, whole)
+            for a in range(4):
+                regroup(g - 1, a)
+            if g == 1:
+                for k in order[1:]:
+                    load_x(k, 3)
+            if g == 2:
+                store_y(0)
+                store_y(1)
+            if g == 3:
+                store_y(2)
+            if g >= 2:
+                interleave(nc.scalar.copy, y_bf[g - 2], y_rows[g - 2])
+            if g + 1 < G:
+                admit(nc.gpsimd, g, whole)
+
+        last = G - 1
+        for cols in halves:
+            admit(nc.vector, last, cols)
+        for cols in halves:
+            new_cell(last, cols)
+            squash(last, cols)
+        for u, cols in enumerate(halves):
+            emit(last, cols)
+            regroup(last, 2 * u)
+            regroup(last, 2 * u + 1)
+        store_y(last)
+        interleave(nc.scalar.copy, y_bf[2], y_rows[2])
+        store_words(0)
+        for g in (1, 2):
+            quantize_y(g)
+            store_words(g)
+        interleave(nc.vector.tensor_copy, y_bf[last], y_rows[last])
+        quantize_y(last)
+        for a in range(4):
+            store_words_quarter(last, a)
+            store_scales(a)

@@ -17,64 +17,73 @@ ALU = mybir.AluOpType
 P = 128
 PACK = 4
 ROWS = D // PACK
-QUARTER = N // 4
 HALF = N // 2
+H_VECTOR_COLS = 336
+Y_VECTOR_COLS = 168
 
 
 def tile_rows_pl_cell_lstm_kernel(tc, h, wi, wf, wo, wc, xi, xf, xo, xc, c, out_0, out_1, out_2):
     nc = tc.nc
     weights = {"f": wf, "i": wi, "c": wc, "o": wo}
-    addends = {"f": xf, "i": xi, "c": xc, "o": xo, "cell": c}
+    addends = {"f": xf, "i": xi, "c": xc, "o": xo}
     bank_of = {"f": 0, "i": 1, "c": 0, "o": 1}
     func_of = {"f": ACT.Sigmoid, "i": ACT.Sigmoid, "c": ACT.Tanh, "o": ACT.Sigmoid}
-    words_hbm = out_1.rearrange("s p n t -> (s p) (n t)").bitcast(I32)
-    scales_hbm = out_2.rearrange("s (g b) n -> (s b) g n", b=4).bitcast(I32)
+    words_hbm = out_1.rearrange("z (s r) n t -> r (z s) (n t)", s=2).bitcast(I32)
+    scales_hbm = out_2.rearrange("z (s e b) n -> (z e) b s n", s=2, e=2).bitcast(I32)
 
     with ExitStack() as ctx:
         keep = ctx.enter_context(tc.tile_pool(name="keep", bufs=1))
         psum = ctx.enter_context(tc.psum_pool(name="psum", bufs=1))
         ctx.enter_context(tc.manual_schedule())
 
-        def sbuf(name, shape, dtype, tag=""):
-            return keep.tile(shape, dtype, name=name, tag=tag or name, align_bytes=64)
+        def sbuf(name, shape, dtype):
+            return keep.tile(shape, dtype, name=name, align_bytes=64)
 
         banks = [[psum.tile([P, N], F32, name="bank%d%d" % (g, b)) for b in range(2)] for g in range(G)]
         w_raw = {k: sbuf("w_raw_" + k, [P, PACK, M], F32) for k in weights}
         w_bf = {k: sbuf("w_bf_" + k, [P, M, PACK], BF16) for k in weights}
         w_codes = {k: sbuf("w_codes_" + k, [P, M], U32) for k in weights}
         w_scales = {k: sbuf("w_scales_" + k, [P, M], U8) for k in weights}
-        h_raw = [sbuf("h_raw%d" % u, [P, PACK, HALF], F32) for u in range(2)]
-        h_bf = [sbuf("h_bf%d" % u, [P, HALF, PACK], BF16) for u in range(2)]
+        h_raw = sbuf("h_raw", [P, PACK, N], F32)
+        h_bf = sbuf("h_bf", [P, N, PACK], BF16)
         h_codes = sbuf("h_codes", [P, N], U32)
         h_scales = sbuf("h_scales", [P, N], U8)
         x_sb = {(k, g): sbuf("x_%s%d" % (k, g), [P, N], F32) for k in addends for g in range(G)}
         pre = {(k, g): sbuf("pre_%s%d" % (k, g), [P, N], F32) for k in weights for g in range(G)}
-        gate = {(k, g): sbuf("gate_%s%d" % (k, g), [P, N], F32) for k in weights for g in range(G)}
+        gates_fi = [sbuf("gates_fi%d" % g, [P, 2, N], F32) for g in range(G)]
+        cell_cand = [sbuf("cell_cand%d" % g, [P, 2, N], F32) for g in range(G)]
+        gate_o = [sbuf("gate_o%d" % g, [P, N], F32) for g in range(G)]
+        terms = [sbuf("terms%d" % s, [P, 2, N], F32) for s in range(2)]
+        last_terms = [sbuf("last_terms%d" % u, [P, 2, HALF], F32) for u in range(2)]
         cell_new = [sbuf("cell_new%d" % g, [P, N], F32) for g in range(G)]
         y = [sbuf("y%d" % g, [P, N], F32) for g in range(G)]
-        y_rows = [sbuf("y_rows%d" % g, [P, PACK, QUARTER], F32) for g in range(G)]
-        y_bf = [sbuf("y_bf%d" % g, [P, QUARTER, PACK], BF16) for g in range(G)]
-        y_codes = [sbuf("y_codes%d" % g, [P, QUARTER], U32) for g in range(G)]
-        y_scales = sbuf("y_scales", [P, G, QUARTER], U8)
-        kept = sbuf("kept", [P, N], F32)
-        scratch = sbuf("scratch", [P, N], F32)
+        y_round = {g: sbuf("y_round%d" % g, [P, N], BF16) for g in (2, 3)}
+        y_rows = [sbuf("y_rows%d" % s, [P, PACK, HALF], dtype) for s, dtype in enumerate((F32, BF16))]
+        y_bf = [sbuf("y_bf%d" % s, [P, HALF, PACK], BF16) for s in range(2)]
+        y_codes = sbuf("y_codes", [P, 2, HALF], U32)
+        y_scales = sbuf("y_scales", [P, 2, HALF], U8)
         warm_in = sbuf("warm_in", [P, 8], F32)
         warm_out = sbuf("warm_out", [P, 8], F32)
+
+        def squashed(g):
+            return terms[(g + 1) % 2][:, 0, :]
+
+        def gate(k, g):
+            return {"f": gates_fi[g][:, 0, :], "i": gates_fi[g][:, 1, :], "c": cell_cand[g][:, 1, :], "o": gate_o[g][:]}[k]
 
         def load_w(k):
             nc.sync.dma_start(out=w_raw[k][:], in_=weights[k].rearrange("g (p j) m -> (g p) j m", j=PACK))
 
-        def load_h(u):
-            rows = h.rearrange("g (p j) n -> (g p) j n", j=PACK)
-            nc.sync.dma_start(out=h_raw[u][:], in_=rows[:, :, u * HALF : (u + 1) * HALF])
-
         def load_x(k, g):
             nc.sync.dma_start(out=x_sb[k, g][:], in_=addends[k][g])
 
-        def interleave(copy, dst, src):
+        def load_cell(g):
+            nc.sync.dma_start(out=cell_cand[g][:, 0, :], in_=c[g])
+
+        def interleave(copy, dst, src, cols):
             copy(
-                out=dst[:].rearrange("p (c i) t -> p c t i", i=4),
-                in_=src[:].rearrange("p t (c i) -> p c t i", i=4),
+                out=dst[:, cols, :].rearrange("p (c i) t -> p c t i", i=4),
+                in_=src[:, :, cols].rearrange("p t (c i) -> p c t i", i=4),
             )
 
         def quantize(codes, scales, src):
@@ -84,10 +93,6 @@ def tile_rows_pl_cell_lstm_kernel(tc, h, wi, wf, wo, wc, xi, xf, xo, xc, c, out_
 
         def quantize_w(k):
             quantize(w_codes[k][:], w_scales[k][:], w_bf[k])
-
-        def quantize_h(u):
-            cols = slice(u * HALF, (u + 1) * HALF)
-            quantize(h_codes[:, cols], h_scales[:, cols], h_bf[u])
 
         def product(k, g):
             rows = slice(ROWS * g, ROWS * (g + 1))
@@ -101,157 +106,143 @@ def tile_rows_pl_cell_lstm_kernel(tc, h, wi, wf, wo, wc, xi, xf, xo, xc, c, out_
                 stop=True,
             )
 
-        def add_input(k, g):
+        def make_gate(k, g):
             nc.vector.tensor_tensor(out=pre[k, g][:], in0=banks[g][bank_of[k]][:], in1=x_sb[k, g][:], op=ALU.add)
+            nc.scalar.activation(out=gate(k, g), in_=pre[k, g][:], func=func_of[k])
 
-        def activate(k, g):
-            nc.scalar.activation(out=gate[k, g][:], in_=pre[k, g][:], func=func_of[k])
-
-        def keep_cell(g):
-            nc.gpsimd.tensor_tensor(out=kept[:], in0=gate["f", g][:], in1=x_sb["cell", g][:], op=ALU.mult)
-
-        def admit(engine, g, cols):
-            engine.tensor_tensor(out=scratch[:, cols], in0=gate["i", g][:, cols], in1=gate["c", g][:, cols], op=ALU.mult)
-
-        def new_cell(g, cols):
-            nc.vector.tensor_tensor(out=cell_new[g][:, cols], in0=kept[:, cols], in1=scratch[:, cols], op=ALU.add)
-
-        def squash(g, cols):
-            nc.scalar.activation(out=scratch[:, cols], in_=cell_new[g][:, cols], func=ACT.Tanh)
-
-        def emit(g, cols):
-            nc.vector.tensor_tensor(out=y[g][:, cols], in0=gate["o", g][:, cols], in1=scratch[:, cols], op=ALU.mult)
-
-        def regroup(g, a):
-            nc.sync.dma_start(
-                out=y_rows[g][ROWS * a : ROWS * (a + 1), :, :], in_=y[g][:, QUARTER * a : QUARTER * (a + 1)]
+        def make_terms(engine, dst, g, rows, cols):
+            engine.tensor_tensor(
+                out=dst, in0=gates_fi[g][:, rows, cols], in1=cell_cand[g][:, rows, cols], op=ALU.mult
             )
+
+        def new_cell(src, g, cols):
+            nc.vector.tensor_tensor(out=cell_new[g][:, cols], in0=src[:, 0, :], in1=src[:, 1, :], op=ALU.add)
+            nc.scalar.activation(out=squashed(g)[:, cols], in_=cell_new[g][:, cols], func=ACT.Tanh)
+
+        def emit(dst, g, cols):
+            nc.vector.tensor_tensor(out=dst[g][:, cols], in0=gate_o[g][:, cols], in1=squashed(g)[:, cols], op=ALU.mult)
+
+        def regroup(engine, src, g, u):
+            q = 2 * u + g % 2
+            engine.dma_start(out=y_rows[g // 2][ROWS * q : ROWS * (q + 1), :, :], in_=src[g][:, halves[u]])
 
         def store_y(g):
             nc.sync.dma_start(out=out_0[M * g : M * (g + 1), :], in_=y[g][:])
 
-        def quantize_y(g):
-            quantize(y_codes[g][:], y_scales[:, g, :], y_bf[g])
+        def quantize_y(s):
+            quantize(y_codes[:, s, :], y_scales[:, s, :], y_bf[s])
 
-        def store_words(g):
-            dst = words_hbm[ROWS * g : ROWS * (g + 1), :].rearrange("p (a n) -> a p n", a=4)
-            nc.sync.dma_start(out=dst, in_=y_codes[g][:].bitcast(I32))
-
-        def store_words_quarter(g, a):
-            nc.sync.dma_start(
-                out=words_hbm[ROWS * g : ROWS * (g + 1), QUARTER * a : QUARTER * (a + 1)],
-                in_=y_codes[g][:].bitcast(I32)[ROWS * a : ROWS * (a + 1), :],
+        def store_words(engine, u):
+            engine.dma_start(
+                out=words_hbm[:, :, halves[u]], in_=y_codes[:].bitcast(I32)[2 * ROWS * u : 2 * ROWS * (u + 1), :, :]
             )
 
-        def store_scales(a):
-            width = QUARTER // 4
-            nc.scalar.dma_start(
-                out=scales_hbm[:, :, width * a : width * (a + 1)],
-                in_=y_scales[:].bitcast(I32)[ROWS * a : ROWS * a + 4, :, :],
+        def store_scales(engine, u, e):
+            q = 2 * u + e
+            width = HALF // 4
+            engine.dma_start(
+                out=scales_hbm[e][:, :, width * u : width * (u + 1)],
+                in_=y_scales[:].bitcast(I32)[ROWS * q : ROWS * q + 4, :, :],
             )
 
         whole = slice(0, N)
         halves = [slice(0, HALF), slice(HALF, N)]
-        order = ["f", "i", "c", "cell", "o"]
+        w_cols = slice(0, M)
+        last = G - 1
+        queues = (nc.sync, nc.scalar)
 
         nc.gpsimd.memset(warm_in[:], 0.0)
         nc.scalar.activation(out=warm_out[:], in_=warm_in[:], func=ACT.Sigmoid)
 
         load_w("f")
-        load_h(0)
-        load_h(1)
+        nc.sync.dma_start(out=h_raw[:], in_=h.rearrange("g (p j) n -> (g p) j n", j=PACK))
         load_w("i")
         load_x("f", 0)
         load_w("c")
         load_x("i", 0)
+        load_x("c", 0)
         load_w("o")
-        for k in order[2:]:
-            load_x(k, 0)
-        for g in (1, 2):
-            for k in order:
-                load_x(k, g)
-        load_x("f", 3)
+        load_x("f", 1)
+        load_x("i", 1)
+        load_cell(0)
+        for g in range(1, G):
+            if g > 1:
+                load_cell(g - 1)
+                load_x("i", g)
+            load_x("o", g - 1)
+            load_x("c", g)
+            load_x(*(("f", g + 1) if g < last else ("o", last)))
+        load_cell(last)
 
-        interleave(nc.vector.tensor_copy, w_bf["f"], w_raw["f"])
+        interleave(nc.vector.tensor_copy, w_bf["f"], w_raw["f"], w_cols)
         quantize_w("f")
-        interleave(nc.vector.tensor_copy, h_bf[0], h_raw[0])
-        quantize_h(0)
-        interleave(nc.vector.tensor_copy, h_bf[1], h_raw[1])
-        interleave(nc.scalar.copy, w_bf["i"], w_raw["i"])
-        quantize_h(1)
+        interleave(nc.vector.tensor_copy, h_bf, h_raw, slice(0, H_VECTOR_COLS))
+        interleave(nc.scalar.copy, h_bf, h_raw, slice(H_VECTOR_COLS, N))
+        interleave(nc.scalar.copy, w_bf["i"], w_raw["i"], w_cols)
+        quantize(h_codes[:], h_scales[:], h_bf)
         quantize_w("i")
         for g in (0, 1):
             product("f", g)
             product("i", g)
 
-        interleave(nc.scalar.copy, w_bf["c"], w_raw["c"])
-        add_input("f", 0)
-        activate("f", 0)
+        interleave(nc.scalar.copy, w_bf["c"], w_raw["c"], w_cols)
+        make_gate("f", 0)
         quantize_w("c")
         product("c", 0)
-        interleave(nc.scalar.copy, w_bf["o"], w_raw["o"])
-        add_input("i", 0)
-        activate("i", 0)
+        interleave(nc.scalar.copy, w_bf["o"], w_raw["o"], w_cols)
+        make_gate("i", 0)
+        make_gate("c", 0)
         quantize_w("o")
         product("o", 0)
-        keep_cell(0)
-        for k in ("c", "o"):
-            add_input(k, 0)
-            activate(k, 0)
-        admit(nc.gpsimd, 0, whole)
+        product("f", 2)
+        product("i", 2)
+        make_gate("f", 1)
+        product("c", 1)
 
         for g in range(1, G):
-            if g + 1 < G:
-                product("f", g + 1)
-                product("i", g + 1)
-            add_input("f", g)
-            activate("f", g)
-            product("c", g)
-            add_input("i", g)
-            activate("i", g)
-            product("o", g)
-            if g == 3:
-                quantize_y(0)
-            new_cell(g - 1, whole)
-            squash(g - 1, whole)
-            keep_cell(g)
-            for k in ("c", "o"):
-                add_input(k, g)
-                activate(k, g)
-            emit(g - 1, whole)
-            for a in range(4):
-                regroup(g - 1, a)
             if g == 1:
-                for k in order[1:]:
-                    load_x(k, 3)
-            if g == 2:
-                store_y(0)
-                store_y(1)
-            if g == 3:
-                store_y(2)
+                for row in range(2):
+                    make_terms(nc.gpsimd, terms[0][:, row, :], 0, row, whole)
+            else:
+                make_terms(nc.gpsimd, terms[(g - 1) // 2][:], g - 1, slice(0, 2), whole)
+            make_gate("i", g)
+            product("o", g)
+            if g == 1:
+                product("f", last)
+                product("i", last)
+            make_gate("o", g - 1)
+            make_gate("c", g)
+            if g < last:
+                make_gate("f", g + 1)
+                product("c", g + 1)
+            else:
+                make_gate("o", last)
             if g >= 2:
-                interleave(nc.scalar.copy, y_bf[g - 2], y_rows[g - 2])
-            if g + 1 < G:
-                admit(nc.gpsimd, g, whole)
+                emit(y, g - 2, whole)
+                regroup(nc.sync, y, g - 2, 0)
+                regroup(nc.sync, y, g - 2, 1)
+                store_y(g - 2)
+            new_cell(terms[(g - 1) // 2], g - 1, whole)
 
-        last = G - 1
-        for cols in halves:
-            admit(nc.vector, last, cols)
-        for cols in halves:
-            new_cell(last, cols)
-            squash(last, cols)
         for u, cols in enumerate(halves):
-            emit(last, cols)
-            regroup(last, 2 * u)
-            regroup(last, 2 * u + 1)
-        store_y(last)
-        interleave(nc.scalar.copy, y_bf[2], y_rows[2])
-        store_words(0)
-        for g in (1, 2):
-            quantize_y(g)
-            store_words(g)
-        interleave(nc.vector.tensor_copy, y_bf[last], y_rows[last])
-        quantize_y(last)
-        for a in range(4):
-            store_words_quarter(last, a)
-            store_scales(a)
+            make_terms(nc.vector, last_terms[u][:], last, slice(0, 2), cols)
+        for u, cols in enumerate(halves):
+            new_cell(last_terms[u], last, cols)
+        emit(y_round, last - 1, whole)
+        for u, engine in enumerate(queues):
+            regroup(engine, y_round, last - 1, u)
+        for u, cols in enumerate(halves):
+            emit(y_round, last, cols)
+            regroup(nc.sync, y_round, last, u)
+        interleave(nc.scalar.copy, y_bf[0], y_rows[0], slice(0, HALF))
+        for g in (last - 1, last):
+            emit(y, g, whole)
+            store_y(g)
+        quantize_y(0)
+        interleave(nc.vector.tensor_copy, y_bf[1], y_rows[1], slice(0, Y_VECTOR_COLS))
+        interleave(nc.scalar.copy, y_bf[1], y_rows[1], slice(Y_VECTOR_COLS, HALF))
+        quantize_y(1)
+        for u, engine in enumerate(queues):
+            store_words(engine, u)
+            store_scales(engine, u, 0)
+            store_scales(engine, u, 1)

@@ -17,8 +17,10 @@ ALU = mybir.AluOpType
 P = 128
 PACK = 4
 ROWS = D // PACK
+BLOCKS = D // 32
 HALF = N // 2
-H_VECTOR_COLS = 336
+RUN = 4
+H_VECTOR_COLS = 368
 Y_VECTOR_COLS = 168
 
 
@@ -26,8 +28,8 @@ def tile_rows_pl_cell_lstm_kernel(tc, h, wi, wf, wo, wc, xi, xf, xo, xc, c, out_
     nc = tc.nc
     weights = {"f": wf, "i": wi, "c": wc, "o": wo}
     addends = {"f": xf, "i": xi, "c": xc, "o": xo}
-    bank_of = {"f": 0, "i": 1, "c": 0, "o": 1}
     func_of = {"f": ACT.Sigmoid, "i": ACT.Sigmoid, "c": ACT.Tanh, "o": ACT.Sigmoid}
+    bank_of = {"f": 0, "i": 1, "c": 0, "o": 1}
     words_hbm = out_1.rearrange("z (s r) n t -> r (z s) (n t)", s=2).bitcast(I32)
     scales_hbm = out_2.rearrange("z (s e b) n -> (z e) b s n", s=2, e=2).bitcast(I32)
 
@@ -36,8 +38,8 @@ def tile_rows_pl_cell_lstm_kernel(tc, h, wi, wf, wo, wc, xi, xf, xo, xc, c, out_
         psum = ctx.enter_context(tc.psum_pool(name="psum", bufs=1))
         ctx.enter_context(tc.manual_schedule())
 
-        def sbuf(name, shape, dtype):
-            return keep.tile(shape, dtype, name=name, align_bytes=64)
+        def sbuf(name, shape, dtype, tag=None):
+            return keep.tile(shape, dtype, name=name, tag=tag or name, align_bytes=64)
 
         banks = [[psum.tile([P, N], F32, name="bank%d%d" % (g, b)) for b in range(2)] for g in range(G)]
         w_raw = {k: sbuf("w_raw_" + k, [P, PACK, M], F32) for k in weights}
@@ -48,12 +50,16 @@ def tile_rows_pl_cell_lstm_kernel(tc, h, wi, wf, wo, wc, xi, xf, xo, xc, c, out_
         h_bf = sbuf("h_bf", [P, N, PACK], BF16)
         h_codes = sbuf("h_codes", [P, N], U32)
         h_scales = sbuf("h_scales", [P, N], U8)
-        x_sb = {(k, g): sbuf("x_%s%d" % (k, g), [P, N], F32) for k in addends for g in range(G)}
+        x_first = {k: sbuf("x_first_" + k, [P, 2, N], F32) for k in ("f", "i")}
+        x_sb = {(k, g): x_first[k][:, g, :] for k in x_first for g in range(2)}
+        for k in addends:
+            for g in range(G):
+                if (k, g) not in x_sb:
+                    x_sb[k, g] = sbuf("x_%s%d" % (k, g), [P, N], F32)[:]
         pre = {(k, g): sbuf("pre_%s%d" % (k, g), [P, N], F32) for k in weights for g in range(G)}
         gates_fi = [sbuf("gates_fi%d" % g, [P, 2, N], F32) for g in range(G)]
         cell_cand = [sbuf("cell_cand%d" % g, [P, 2, N], F32) for g in range(G)]
         gate_o = [sbuf("gate_o%d" % g, [P, N], F32) for g in range(G)]
-        terms = [sbuf("terms%d" % s, [P, 2, N], F32) for s in range(2)]
         last_terms = [sbuf("last_terms%d" % u, [P, 2, HALF], F32) for u in range(2)]
         cell_new = [sbuf("cell_new%d" % g, [P, N], F32) for g in range(G)]
         y = [sbuf("y%d" % g, [P, N], F32) for g in range(G)]
@@ -62,37 +68,46 @@ def tile_rows_pl_cell_lstm_kernel(tc, h, wi, wf, wo, wc, xi, xf, xo, xc, c, out_
         y_bf = [sbuf("y_bf%d" % s, [P, HALF, PACK], BF16) for s in range(2)]
         y_codes = sbuf("y_codes", [P, 2, HALF], U32)
         y_scales = sbuf("y_scales", [P, 2, HALF], U8)
-        warm_in = sbuf("warm_in", [P, 8], F32)
-        warm_out = sbuf("warm_out", [P, 8], F32)
 
-        def squashed(g):
-            return terms[(g + 1) % 2][:, 0, :]
+        whole = slice(0, N)
+        halves = [slice(0, HALF), slice(HALF, N)]
+        last = G - 1
+        queues = (nc.sync, nc.scalar)
 
         def gate(k, g):
-            return {"f": gates_fi[g][:, 0, :], "i": gates_fi[g][:, 1, :], "c": cell_cand[g][:, 1, :], "o": gate_o[g][:]}[k]
+            if k == "o":
+                return gate_o[g][:]
+            return cell_cand[g][:, 1, :] if k == "c" else gates_fi[g][:, "fi".index(k), :]
 
         def load_w(k):
-            nc.sync.dma_start(out=w_raw[k][:], in_=weights[k].rearrange("g (p j) m -> (g p) j m", j=PACK))
+            nc.sync.dma_start(out=w_raw[k][:], in_=weights[k].rearrange("g (p t) m -> (g p) t m", t=PACK))
+
+        def load_x_first(k):
+            nc.sync.dma_start(out=x_first[k][:], in_=addends[k][0:2].rearrange("g m n -> m g n"))
 
         def load_x(k, g):
-            nc.sync.dma_start(out=x_sb[k, g][:], in_=addends[k][g])
+            nc.sync.dma_start(out=x_sb[k, g], in_=addends[k][g])
 
         def load_cell(g):
             nc.sync.dma_start(out=cell_cand[g][:, 0, :], in_=c[g])
 
         def interleave(copy, dst, src, cols):
             copy(
-                out=dst[:, cols, :].rearrange("p (c i) t -> p c t i", i=4),
-                in_=src[:, :, cols].rearrange("p t (c i) -> p c t i", i=4),
+                out=dst[:, cols, :].rearrange("p (a i) t -> p a t i", i=RUN),
+                in_=src[:, :, cols].rearrange("p t (a i) -> p a t i", i=RUN),
             )
 
+        def interleave_w(copy, k):
+            interleave(copy, w_bf[k], w_raw[k], slice(0, M))
+
         def quantize(codes, scales, src):
-            nc.vector.quantize_mx(
-                out=codes.bitcast(FP8X4), scales=scales, in_=src[:].rearrange("p n t -> p (n t)")
-            )
+            nc.vector.quantize_mx(out=codes.bitcast(FP8X4), scales=scales, in_=src[:].rearrange("p n t -> p (n t)"))
 
         def quantize_w(k):
             quantize(w_codes[k][:], w_scales[k][:], w_bf[k])
+
+        def quantize_y(s):
+            quantize(y_codes[:, s, :], y_scales[:, s, :], y_bf[s])
 
         def product(k, g):
             rows = slice(ROWS * g, ROWS * (g + 1))
@@ -107,104 +122,86 @@ def tile_rows_pl_cell_lstm_kernel(tc, h, wi, wf, wo, wc, xi, xf, xo, xc, c, out_
             )
 
         def make_gate(k, g):
-            nc.vector.tensor_tensor(out=pre[k, g][:], in0=banks[g][bank_of[k]][:], in1=x_sb[k, g][:], op=ALU.add)
+            nc.vector.tensor_tensor(out=pre[k, g][:], in0=banks[g][bank_of[k]][:], in1=x_sb[k, g], op=ALU.add)
             nc.scalar.activation(out=gate(k, g), in_=pre[k, g][:], func=func_of[k])
 
         def make_terms(engine, dst, g, rows, cols):
-            engine.tensor_tensor(
-                out=dst, in0=gates_fi[g][:, rows, cols], in1=cell_cand[g][:, rows, cols], op=ALU.mult
-            )
+            engine.tensor_tensor(out=dst, in0=gates_fi[g][:, rows, cols], in1=cell_cand[g][:, rows, cols], op=ALU.mult)
 
-        def new_cell(src, g, cols):
-            nc.vector.tensor_tensor(out=cell_new[g][:, cols], in0=src[:, 0, :], in1=src[:, 1, :], op=ALU.add)
-            nc.scalar.activation(out=squashed(g)[:, cols], in_=cell_new[g][:, cols], func=ACT.Tanh)
+        def new_cell(terms, g, cols):
+            nc.vector.tensor_tensor(out=cell_new[g][:, cols], in0=terms[:, 0, :], in1=terms[:, 1, :], op=ALU.add)
+            nc.scalar.activation(out=tanh_cell(g)[:, cols], in_=cell_new[g][:, cols], func=ACT.Tanh)
 
         def emit(dst, g, cols):
-            nc.vector.tensor_tensor(out=dst[g][:, cols], in0=gate_o[g][:, cols], in1=squashed(g)[:, cols], op=ALU.mult)
+            nc.vector.tensor_tensor(out=dst[g][:, cols], in0=gate_o[g][:, cols], in1=tanh_cell(g)[:, cols], op=ALU.mult)
 
-        def regroup(engine, src, g, u):
+        def regroup(queue, src, g, u):
             q = 2 * u + g % 2
-            engine.dma_start(out=y_rows[g // 2][ROWS * q : ROWS * (q + 1), :, :], in_=src[g][:, halves[u]])
+            queue.dma_start(out=y_rows[g // 2][ROWS * q : ROWS * (q + 1), :, :], in_=src[g][:, halves[u]])
 
         def store_y(g):
             nc.sync.dma_start(out=out_0[M * g : M * (g + 1), :], in_=y[g][:])
 
-        def quantize_y(s):
-            quantize(y_codes[:, s, :], y_scales[:, s, :], y_bf[s])
+        def store_words(queue, s, u):
+            src = y_codes[:].bitcast(I32)[2 * ROWS * u : 2 * ROWS * (u + 1), s, :]
+            queue.dma_start(out=words_hbm[:, s, halves[u]], in_=src)
 
-        def store_words(engine, u):
-            engine.dma_start(
-                out=words_hbm[:, :, halves[u]], in_=y_codes[:].bitcast(I32)[2 * ROWS * u : 2 * ROWS * (u + 1), :, :]
-            )
-
-        def store_scales(engine, u, e):
-            q = 2 * u + e
+        def store_scales(queue, u, e):
+            first = ROWS * (2 * u + e)
             width = HALF // 4
-            engine.dma_start(
-                out=scales_hbm[e][:, :, width * u : width * (u + 1)],
-                in_=y_scales[:].bitcast(I32)[ROWS * q : ROWS * q + 4, :, :],
-            )
+            src = y_scales[:].bitcast(I32)[first : first + BLOCKS, :, :]
+            queue.dma_start(out=scales_hbm[e][:, :, width * u : width * (u + 1)], in_=src)
 
-        whole = slice(0, N)
-        halves = [slice(0, HALF), slice(HALF, N)]
-        w_cols = slice(0, M)
-        last = G - 1
-        queues = (nc.sync, nc.scalar)
-
-        nc.gpsimd.memset(warm_in[:], 0.0)
-        nc.scalar.activation(out=warm_out[:], in_=warm_in[:], func=ACT.Sigmoid)
-
-        load_w("f")
-        nc.sync.dma_start(out=h_raw[:], in_=h.rearrange("g (p j) n -> (g p) j n", j=PACK))
-        load_w("i")
-        load_x("f", 0)
-        load_w("c")
-        load_x("i", 0)
-        load_x("c", 0)
+        nc.sync.dma_start(out=h_raw[:], in_=h.rearrange("g (p t) n -> (g p) t n", t=PACK))
+        for k in ("f", "i", "c"):
+            load_w(k)
+        load_x_first("f")
         load_w("o")
-        load_x("f", 1)
-        load_x("i", 1)
-        load_cell(0)
+        load_x_first("i")
+        load_x("c", 0)
         for g in range(1, G):
+            load_cell(g - 1)
             if g > 1:
-                load_cell(g - 1)
                 load_x("i", g)
             load_x("o", g - 1)
             load_x("c", g)
             load_x(*(("f", g + 1) if g < last else ("o", last)))
         load_cell(last)
 
-        interleave(nc.vector.tensor_copy, w_bf["f"], w_raw["f"], w_cols)
-        quantize_w("f")
         interleave(nc.vector.tensor_copy, h_bf, h_raw, slice(0, H_VECTOR_COLS))
         interleave(nc.scalar.copy, h_bf, h_raw, slice(H_VECTOR_COLS, N))
-        interleave(nc.scalar.copy, w_bf["i"], w_raw["i"], w_cols)
+        for k in ("f", "i"):
+            interleave_w(nc.scalar.copy, k)
         quantize(h_codes[:], h_scales[:], h_bf)
-        quantize_w("i")
-        for g in (0, 1):
-            product("f", g)
-            product("i", g)
-
-        interleave(nc.scalar.copy, w_bf["c"], w_raw["c"], w_cols)
-        make_gate("f", 0)
+        for k in ("f", "i"):
+            quantize_w(k)
+            for g in (0, 1):
+                product(k, g)
+        interleave_w(nc.vector.tensor_copy, "c")
         quantize_w("c")
-        product("c", 0)
-        interleave(nc.scalar.copy, w_bf["o"], w_raw["o"], w_cols)
-        make_gate("i", 0)
-        make_gate("c", 0)
+        for g in (0, 1):
+            make_gate("f", g)
+            product("c", g)
+        interleave_w(nc.vector.tensor_copy, "o")
         quantize_w("o")
-        product("o", 0)
         product("f", 2)
         product("i", 2)
-        make_gate("f", 1)
-        product("c", 1)
+        make_gate("i", 0)
+        product("o", 0)
+        make_gate("c", 0)
+
+        turns = [sbuf("turns0", [P, 2, N], F32, tag="w_bf_o"), sbuf("turns1", [P, 2, N], F32)]
+
+        def tanh_cell(g):
+            return turns[(g + 1) % 2][:, 0, :]
 
         for g in range(1, G):
+            terms = turns[(g - 1) // 2]
             if g == 1:
                 for row in range(2):
-                    make_terms(nc.gpsimd, terms[0][:, row, :], 0, row, whole)
+                    make_terms(nc.gpsimd, terms[:, row, :], 0, row, whole)
             else:
-                make_terms(nc.gpsimd, terms[(g - 1) // 2][:], g - 1, slice(0, 2), whole)
+                make_terms(nc.gpsimd, terms[:], g - 1, slice(0, 2), whole)
             make_gate("i", g)
             product("o", g)
             if g == 1:
@@ -219,30 +216,32 @@ def tile_rows_pl_cell_lstm_kernel(tc, h, wi, wf, wo, wc, xi, xf, xo, xc, c, out_
                 make_gate("o", last)
             if g >= 2:
                 emit(y, g - 2, whole)
-                regroup(nc.sync, y, g - 2, 0)
-                regroup(nc.sync, y, g - 2, 1)
+                for u in range(2):
+                    regroup(nc.sync, y, g - 2, u)
                 store_y(g - 2)
-            new_cell(terms[(g - 1) // 2], g - 1, whole)
+            new_cell(terms, g - 1, whole)
 
         for u, cols in enumerate(halves):
             make_terms(nc.vector, last_terms[u][:], last, slice(0, 2), cols)
         for u, cols in enumerate(halves):
             new_cell(last_terms[u], last, cols)
         emit(y_round, last - 1, whole)
-        for u, engine in enumerate(queues):
-            regroup(engine, y_round, last - 1, u)
+        for u in range(2):
+            regroup(queues[u], y_round, last - 1, u)
         for u, cols in enumerate(halves):
             emit(y_round, last, cols)
-            regroup(nc.sync, y_round, last, u)
+            regroup(queues[1 - u], y_round, last, u)
         interleave(nc.scalar.copy, y_bf[0], y_rows[0], slice(0, HALF))
         for g in (last - 1, last):
             emit(y, g, whole)
             store_y(g)
         quantize_y(0)
+        for u in range(2):
+            store_words(nc.sync, 0, u)
         interleave(nc.vector.tensor_copy, y_bf[1], y_rows[1], slice(0, Y_VECTOR_COLS))
         interleave(nc.scalar.copy, y_bf[1], y_rows[1], slice(Y_VECTOR_COLS, HALF))
         quantize_y(1)
-        for u, engine in enumerate(queues):
-            store_words(engine, u)
-            store_scales(engine, u, 0)
-            store_scales(engine, u, 1)
+        for u, queue in enumerate(queues):
+            store_words(queue, 1, u)
+            for e in range(2):
+                store_scales(queue, u, e)

@@ -22,6 +22,7 @@ HALF = N // 2
 RUN = 4
 H_VECTOR_COLS = 368
 Y_VECTOR_COLS = 168
+GPSIMD_COLS = {1: 400, 2: 208}
 
 
 def tile_rows_pl_cell_lstm_kernel(tc, h, wi, wf, wo, wc, xi, xf, xo, xc, c, out_0, out_1, out_2):
@@ -30,6 +31,7 @@ def tile_rows_pl_cell_lstm_kernel(tc, h, wi, wf, wo, wc, xi, xf, xo, xc, c, out_
     addends = {"f": xf, "i": xi, "c": xc, "o": xo}
     func_of = {"f": ACT.Sigmoid, "i": ACT.Sigmoid, "c": ACT.Tanh, "o": ACT.Sigmoid}
     bank_of = {"f": 0, "i": 1, "c": 0, "o": 1}
+    follower = {"f": "c", "i": "o"}
     words_hbm = out_1.rearrange("z (s r) n t -> r (z s) (n t)", s=2).bitcast(I32)
     scales_hbm = out_2.rearrange("z (s e b) n -> (z e) b s n", s=2, e=2).bitcast(I32)
 
@@ -68,6 +70,8 @@ def tile_rows_pl_cell_lstm_kernel(tc, h, wi, wf, wo, wc, xi, xf, xo, xc, c, out_
         y_bf = [sbuf("y_bf%d" % s, [P, HALF, PACK], BF16) for s in range(2)]
         y_codes = sbuf("y_codes", [P, 2, HALF], U32)
         y_scales = sbuf("y_scales", [P, 2, HALF], U8)
+        warm_in = sbuf("warm_in", [P, 8], F32)
+        warm_out = sbuf("warm_out", [P, 8], F32)
 
         whole = slice(0, N)
         halves = [slice(0, HALF), slice(HALF, N)]
@@ -97,9 +101,6 @@ def tile_rows_pl_cell_lstm_kernel(tc, h, wi, wf, wo, wc, xi, xf, xo, xc, c, out_
                 in_=src[:, :, cols].rearrange("p t (a i) -> p a t i", i=RUN),
             )
 
-        def interleave_w(copy, k):
-            interleave(copy, w_bf[k], w_raw[k], slice(0, M))
-
         def quantize(codes, scales, src):
             nc.vector.quantize_mx(out=codes.bitcast(FP8X4), scales=scales, in_=src[:].rearrange("p n t -> p (n t)"))
 
@@ -128,6 +129,9 @@ def tile_rows_pl_cell_lstm_kernel(tc, h, wi, wf, wo, wc, xi, xf, xo, xc, c, out_
         def make_terms(engine, dst, g, rows, cols):
             engine.tensor_tensor(out=dst, in0=gates_fi[g][:, rows, cols], in1=cell_cand[g][:, rows, cols], op=ALU.mult)
 
+        def flat(tile):
+            return tile[:].rearrange("p r n -> p (r n)")
+
         def new_cell(terms, g, cols):
             nc.vector.tensor_tensor(out=cell_new[g][:, cols], in0=terms[:, 0, :], in1=terms[:, 1, :], op=ALU.add)
             nc.scalar.activation(out=tanh_cell(g)[:, cols], in_=cell_new[g][:, cols], func=ACT.Tanh)
@@ -152,6 +156,15 @@ def tile_rows_pl_cell_lstm_kernel(tc, h, wi, wf, wo, wc, xi, xf, xo, xc, c, out_
             src = y_scales[:].bitcast(I32)[first : first + BLOCKS, :, :]
             queue.dma_start(out=scales_hbm[e][:, :, width * u : width * (u + 1)], in_=src)
 
+        nc.gpsimd.memset(warm_in[:], 0.0)
+        nc.scalar.activation(out=warm_out[:], in_=warm_in[:], func=ACT.Sigmoid)
+
+        runs = [
+            [("i", 1), ("o", 0), ("c", 1), ("f", 2), ("i", 2)],
+            [("o", 1), ("c", 2), ("f", 3), ("i", 3)],
+            [("c", 3), ("o", 2), ("o", 3)],
+        ]
+
         nc.sync.dma_start(out=h_raw[:], in_=h.rearrange("g (p t) n -> (g p) t n", t=PACK))
         for k in ("f", "i", "c"):
             load_w(k)
@@ -159,35 +172,33 @@ def tile_rows_pl_cell_lstm_kernel(tc, h, wi, wf, wo, wc, xi, xf, xo, xc, c, out_
         load_w("o")
         load_x_first("i")
         load_x("c", 0)
-        for g in range(1, G):
-            load_cell(g - 1)
-            if g > 1:
-                load_x("i", g)
-            load_x("o", g - 1)
-            load_x("c", g)
-            load_x(*(("f", g + 1) if g < last else ("o", last)))
+        for g, run in enumerate(runs):
+            load_cell(g)
+            for k, head in run:
+                if (k, head) != ("i", 1):
+                    load_x(k, head)
         load_cell(last)
 
         interleave(nc.vector.tensor_copy, h_bf, h_raw, slice(0, H_VECTOR_COLS))
         interleave(nc.scalar.copy, h_bf, h_raw, slice(H_VECTOR_COLS, N))
-        for k in ("f", "i"):
-            interleave_w(nc.scalar.copy, k)
+        for k in weights:
+            interleave(nc.scalar.copy, w_bf[k], w_raw[k], slice(0, M))
         quantize(h_codes[:], h_scales[:], h_bf)
         for k in ("f", "i"):
             quantize_w(k)
             for g in (0, 1):
                 product(k, g)
-        interleave_w(nc.vector.tensor_copy, "c")
         quantize_w("c")
         for g in (0, 1):
             make_gate("f", g)
             product("c", g)
-        interleave_w(nc.vector.tensor_copy, "o")
         quantize_w("o")
         product("f", 2)
         product("i", 2)
         make_gate("i", 0)
         product("o", 0)
+        product("f", last)
+        product("i", last)
         make_gate("c", 0)
 
         turns = [sbuf("turns0", [P, 2, N], F32, tag="w_bf_o"), sbuf("turns1", [P, 2, N], F32)]
@@ -195,31 +206,28 @@ def tile_rows_pl_cell_lstm_kernel(tc, h, wi, wf, wo, wc, xi, xf, xo, xc, c, out_
         def tanh_cell(g):
             return turns[(g + 1) % 2][:, 0, :]
 
-        for g in range(1, G):
-            terms = turns[(g - 1) // 2]
-            if g == 1:
+        for g, run in enumerate(runs):
+            terms = turns[g // 2]
+            if g == 0:
                 for row in range(2):
-                    make_terms(nc.gpsimd, terms[:, row, :], 0, row, whole)
+                    make_terms(nc.gpsimd, terms[:, row, :], g, row, whole)
             else:
-                make_terms(nc.gpsimd, terms[:], g - 1, slice(0, 2), whole)
-            make_gate("i", g)
-            product("o", g)
-            if g == 1:
-                product("f", last)
-                product("i", last)
-            make_gate("o", g - 1)
-            make_gate("c", g)
-            if g < last:
-                make_gate("f", g + 1)
-                product("c", g + 1)
-            else:
-                make_gate("o", last)
-            if g >= 2:
-                emit(y, g - 2, whole)
+                share = slice(0, N + GPSIMD_COLS[g])
+                nc.gpsimd.tensor_tensor(
+                    out=flat(terms)[:, share], in0=flat(gates_fi[g])[:, share], in1=flat(cell_cand[g])[:, share], op=ALU.mult
+                )
+            for k, head in run:
+                make_gate(k, head)
+                if k in follower:
+                    product(follower[k], head)
+            if g > 0:
+                rest = slice(GPSIMD_COLS[g], N)
+                make_terms(nc.vector, terms[:, 1, rest], g, 1, rest)
+                emit(y, g - 1, whole)
                 for u in range(2):
-                    regroup(nc.sync, y, g - 2, u)
-                store_y(g - 2)
-            new_cell(terms, g - 1, whole)
+                    regroup(nc.sync, y, g - 1, u)
+                store_y(g - 1)
+            new_cell(terms, g, whole)
 
         for u, cols in enumerate(halves):
             make_terms(nc.vector, last_terms[u][:], last, slice(0, 2), cols)

from contextlib import ExitStack

import concourse.mybir as mybir

G, D, M, N = 4, 128, 128, 512
FLOPS = 2 * 4 * G * D * M * N

F32 = mybir.dt.float32
BF16 = mybir.dt.bfloat16
U32 = mybir.dt.uint32
I32 = mybir.dt.int32
U8 = mybir.dt.uint8
FP8X4 = mybir.dt.float8_e4m3fn_x4
ACT = mybir.ActivationFunctionType
ALU = mybir.AluOpType

P = 128
PACK = 4
ROWS = D // PACK
BLOCKS = D // 32
HALF = N // 2
RUN = 4
H_VECTOR_COLS = 368
Y_VECTOR_COLS = 168
GPSIMD_COLS = {1: 400, 2: 208}


def tile_rows_pl_cell_lstm_kernel(tc, h, wi, wf, wo, wc, xi, xf, xo, xc, c, out_0, out_1, out_2):
    nc = tc.nc
    weights = {"f": wf, "i": wi, "c": wc, "o": wo}
    addends = {"f": xf, "i": xi, "c": xc, "o": xo}
    func_of = {"f": ACT.Sigmoid, "i": ACT.Sigmoid, "c": ACT.Tanh, "o": ACT.Sigmoid}
    bank_of = {"f": 0, "i": 1, "c": 0, "o": 1}
    follower = {"f": "c", "i": "o"}
    words_hbm = out_1.rearrange("z (s r) n t -> r (z s) (n t)", s=2).bitcast(I32)
    scales_hbm = out_2.rearrange("z (s e b) n -> (z e) b s n", s=2, e=2).bitcast(I32)

    with ExitStack() as ctx:
        keep = ctx.enter_context(tc.tile_pool(name="keep", bufs=1))
        psum = ctx.enter_context(tc.psum_pool(name="psum", bufs=1))
        ctx.enter_context(tc.manual_schedule())

        def sbuf(name, shape, dtype, tag=None):
            return keep.tile(shape, dtype, name=name, tag=tag or name, align_bytes=64)

        banks = [[psum.tile([P, N], F32, name="bank%d%d" % (g, b)) for b in range(2)] for g in range(G)]
        w_raw = {k: sbuf("w_raw_" + k, [P, PACK, M], F32) for k in weights}
        w_bf = {k: sbuf("w_bf_" + k, [P, M, PACK], BF16) for k in weights}
        w_codes = {k: sbuf("w_codes_" + k, [P, M], U32) for k in weights}
        w_scales = {k: sbuf("w_scales_" + k, [P, M], U8) for k in weights}
        h_raw = sbuf("h_raw", [P, PACK, N], F32)
        h_bf = sbuf("h_bf", [P, N, PACK], BF16)
        h_codes = sbuf("h_codes", [P, N], U32)
        h_scales = sbuf("h_scales", [P, N], U8)
        x_first = {k: sbuf("x_first_" + k, [P, 2, N], F32) for k in ("f", "i")}
        x_sb = {(k, g): x_first[k][:, g, :] for k in x_first for g in range(2)}
        for k in addends:
            for g in range(G):
                if (k, g) not in x_sb:
                    x_sb[k, g] = sbuf("x_%s%d" % (k, g), [P, N], F32)[:]
        pre = {(k, g): sbuf("pre_%s%d" % (k, g), [P, N], F32) for k in weights for g in range(G)}
        gates_fi = [sbuf("gates_fi%d" % g, [P, 2, N], F32) for g in range(G)]
        cell_cand = [sbuf("cell_cand%d" % g, [P, 2, N], F32) for g in range(G)]
        gate_o = [sbuf("gate_o%d" % g, [P, N], F32) for g in range(G)]
        last_terms = [sbuf("last_terms%d" % u, [P, 2, HALF], F32) for u in range(2)]
        cell_new = [sbuf("cell_new%d" % g, [P, N], F32) for g in range(G)]
        y = [sbuf("y%d" % g, [P, N], F32) for g in range(G)]
        y_round = {g: sbuf("y_round%d" % g, [P, N], BF16) for g in (2, 3)}
        y_rows = [sbuf("y_rows%d" % s, [P, PACK, HALF], dtype) for s, dtype in enumerate((F32, BF16))]
        y_bf = [sbuf("y_bf%d" % s, [P, HALF, PACK], BF16) for s in range(2)]
        y_codes = sbuf("y_codes", [P, 2, HALF], U32)
        y_scales = sbuf("y_scales", [P, 2, HALF], U8)
        warm_in = sbuf("warm_in", [P, 8], F32)
        warm_out = sbuf("warm_out", [P, 8], F32)

        whole = slice(0, N)
        halves = [slice(0, HALF), slice(HALF, N)]
        last = G - 1
        queues = (nc.sync, nc.scalar)

        def gate(k, g):
            if k == "o":
                return gate_o[g][:]
            return cell_cand[g][:, 1, :] if k == "c" else gates_fi[g][:, "fi".index(k), :]

        def load_w(k):
            nc.sync.dma_start(out=w_raw[k][:], in_=weights[k].rearrange("g (p t) m -> (g p) t m", t=PACK))

        def load_x_first(k):
            nc.sync.dma_start(out=x_first[k][:], in_=addends[k][0:2].rearrange("g m n -> m g n"))

        def load_x(k, g):
            nc.sync.dma_start(out=x_sb[k, g], in_=addends[k][g])

        def load_cell(g):
            nc.sync.dma_start(out=cell_cand[g][:, 0, :], in_=c[g])

        def interleave(copy, dst, src, cols):
            copy(
                out=dst[:, cols, :].rearrange("p (a i) t -> p a t i", i=RUN),
                in_=src[:, :, cols].rearrange("p t (a i) -> p a t i", i=RUN),
            )

        def quantize(codes, scales, src):
            nc.vector.quantize_mx(out=codes.bitcast(FP8X4), scales=scales, in_=src[:].rearrange("p n t -> p (n t)"))

        def quantize_w(k):
            quantize(w_codes[k][:], w_scales[k][:], w_bf[k])

        def quantize_y(s):
            quantize(y_codes[:, s, :], y_scales[:, s, :], y_bf[s])

        def product(k, g):
            rows = slice(ROWS * g, ROWS * (g + 1))
            nc.tensor.matmul_mx(
                out=banks[g][bank_of[k]][:],
                lhsT=w_codes[k][rows, :].bitcast(FP8X4),
                lhsT_scale=w_scales[k][rows, :],
                rhs=h_codes[rows, :].bitcast(FP8X4),
                rhs_scale=h_scales[rows, :],
                start=True,
                stop=True,
            )

        def make_gate(k, g):
            nc.vector.tensor_tensor(out=pre[k, g][:], in0=banks[g][bank_of[k]][:], in1=x_sb[k, g], op=ALU.add)
            nc.scalar.activation(out=gate(k, g), in_=pre[k, g][:], func=func_of[k])

        def make_terms(engine, dst, g, rows, cols):
            engine.tensor_tensor(out=dst, in0=gates_fi[g][:, rows, cols], in1=cell_cand[g][:, rows, cols], op=ALU.mult)

        def flat(tile):
            return tile[:].rearrange("p r n -> p (r n)")

        def new_cell(terms, g, cols):
            nc.vector.tensor_tensor(out=cell_new[g][:, cols], in0=terms[:, 0, :], in1=terms[:, 1, :], op=ALU.add)
            nc.scalar.activation(out=tanh_cell(g)[:, cols], in_=cell_new[g][:, cols], func=ACT.Tanh)

        def emit(dst, g, cols):
            nc.vector.tensor_tensor(out=dst[g][:, cols], in0=gate_o[g][:, cols], in1=tanh_cell(g)[:, cols], op=ALU.mult)

        def regroup(queue, src, g, u):
            q = 2 * u + g % 2
            queue.dma_start(out=y_rows[g // 2][ROWS * q : ROWS * (q + 1), :, :], in_=src[g][:, halves[u]])

        def store_y(g):
            nc.sync.dma_start(out=out_0[M * g : M * (g + 1), :], in_=y[g][:])

        def store_words(queue, s, u):
            src = y_codes[:].bitcast(I32)[2 * ROWS * u : 2 * ROWS * (u + 1), s, :]
            queue.dma_start(out=words_hbm[:, s, halves[u]], in_=src)

        def store_scales(queue, u, e):
            first = ROWS * (2 * u + e)
            width = HALF // 4
            src = y_scales[:].bitcast(I32)[first : first + BLOCKS, :, :]
            queue.dma_start(out=scales_hbm[e][:, :, width * u : width * (u + 1)], in_=src)

        nc.gpsimd.memset(warm_in[:], 0.0)
        nc.scalar.activation(out=warm_out[:], in_=warm_in[:], func=ACT.Sigmoid)

        runs = [
            [("i", 1), ("o", 0), ("c", 1), ("f", 2), ("i", 2)],
            [("o", 1), ("c", 2), ("f", 3), ("i", 3)],
            [("c", 3), ("o", 2), ("o", 3)],
        ]

        nc.sync.dma_start(out=h_raw[:], in_=h.rearrange("g (p t) n -> (g p) t n", t=PACK))
        for k in ("f", "i", "c"):
            load_w(k)
        load_x_first("f")
        load_w("o")
        load_x_first("i")
        load_x("c", 0)
        for g, run in enumerate(runs):
            load_cell(g)
            for k, head in run:
                if (k, head) != ("i", 1):
                    load_x(k, head)
        load_cell(last)

        interleave(nc.vector.tensor_copy, h_bf, h_raw, slice(0, H_VECTOR_COLS))
        interleave(nc.scalar.copy, h_bf, h_raw, slice(H_VECTOR_COLS, N))
        for k in weights:
            interleave(nc.scalar.copy, w_bf[k], w_raw[k], slice(0, M))
        quantize(h_codes[:], h_scales[:], h_bf)
        for k in ("f", "i"):
            quantize_w(k)
            for g in (0, 1):
                product(k, g)
        quantize_w("c")
        for g in (0, 1):
            make_gate("f", g)
            product("c", g)
        quantize_w("o")
        product("f", 2)
        product("i", 2)
        make_gate("i", 0)
        product("o", 0)
        product("f", last)
        product("i", last)
        make_gate("c", 0)

        turns = [sbuf("turns0", [P, 2, N], F32, tag="w_bf_o"), sbuf("turns1", [P, 2, N], F32)]

        def tanh_cell(g):
            return turns[(g + 1) % 2][:, 0, :]

        for g, run in enumerate(runs):
            terms = turns[g // 2]
            if g == 0:
                for row in range(2):
                    make_terms(nc.gpsimd, terms[:, row, :], g, row, whole)
            else:
                share = slice(0, N + GPSIMD_COLS[g])
                nc.gpsimd.tensor_tensor(
                    out=flat(terms)[:, share], in0=flat(gates_fi[g])[:, share], in1=flat(cell_cand[g])[:, share], op=ALU.mult
                )
            for k, head in run:
                make_gate(k, head)
                if k in follower:
                    product(follower[k], head)
            if g > 0:
                rest = slice(GPSIMD_COLS[g], N)
                make_terms(nc.vector, terms[:, 1, rest], g, 1, rest)
                emit(y, g - 1, whole)
                for u in range(2):
                    regroup(nc.sync, y, g - 1, u)
                store_y(g - 1)
            new_cell(terms, g, whole)

        for u, cols in enumerate(halves):
            make_terms(nc.vector, last_terms[u][:], last, slice(0, 2), cols)
        for u, cols in enumerate(halves):
            new_cell(last_terms[u], last, cols)
        emit(y_round, last - 1, whole)
        for u in range(2):
            regroup(queues[u], y_round, last - 1, u)
        for u, cols in enumerate(halves):
            emit(y_round, last, cols)
            regroup(queues[1 - u], y_round, last, u)
        interleave(nc.scalar.copy, y_bf[0], y_rows[0], slice(0, HALF))
        for g in (last - 1, last):
            emit(y, g, whole)
            store_y(g)
        quantize_y(0)
        for u in range(2):
            store_words(nc.sync, 0, u)
        interleave(nc.vector.tensor_copy, y_bf[1], y_rows[1], slice(0, Y_VECTOR_COLS))
        interleave(nc.scalar.copy, y_bf[1], y_rows[1], slice(Y_VECTOR_COLS, HALF))
        quantize_y(1)
        for u, queue in enumerate(queues):
            store_words(queue, 1, u)
            for e in range(2):
                store_scales(queue, u, e)
